import numpy as np
import ml_dtypes


def mxq(x, axis, fmt="e4m3"):
    dtype, down = {"e4m3": (ml_dtypes.float8_e4m3fn, 7), "e5m2": (ml_dtypes.float8_e5m2, 14)}[fmt]
    v = np.moveaxis(np.asarray(x, np.float32).astype(ml_dtypes.bfloat16).astype(np.float64), axis, -1)
    blocks = v.reshape(v.shape[:-1] + (-1, 32))
    amax = np.abs(blocks).max(-1, keepdims=True)
    byte = np.maximum(np.where(amax > 0, np.frexp(amax)[1] - 1 + 127, 0) - down, 1)
    scale = np.exp2(byte - 127.0)
    codes = (blocks / scale).astype(np.float32).astype(dtype).astype(np.float64)
    return np.moveaxis((codes * scale).reshape(v.shape), -1, axis)


WIDE = False


def mx_kscale(k):
    if not WIDE:
        return np.ones(k)
    levels = np.array([10, -10, 5, -5, 0])
    if k % 512:
        return np.exp2(np.random.permutation(np.resize(levels, k // 32))).repeat(32)
    a = np.empty((k // 512, 16))
    for p in range(k // 512):
        a[p, :8] = np.random.permutation(np.resize(levels, 8))
        for g in range(8):
            far = levels[np.abs(levels - a[p, g]) >= 10]
            a[p, g + 8] = far[np.random.randint(len(far))]
    return np.exp2(a.ravel()).repeat(32)


def f64(x):
    return np.asarray(x).astype(np.float64)


def striped(idx):
    return np.tile(idx.reshape(-1, 16).T, (8, 1)).astype(np.uint16)


def unstriped(offs):
    return offs[:16].T.reshape(-1).astype(np.int64)


E2M1 = np.array([0.0, 0.5, 1.0, 1.5, 2.0, 3.0, 4.0, 6.0, -0.0, -0.5, -1.0, -1.5, -2.0, -3.0, -4.0, -6.0])


def pack_weight(w, fmt):
    k, n = w.shape
    w = f64(np.asarray(w, np.float32).astype(ml_dtypes.bfloat16)).reshape(k // 32, 32, n)
    amax = np.abs(w).max(1)
    if fmt == "e4m3":
        byte = np.frexp(amax)[1] - 1 + 127 - 7
    else:
        mant, ex = np.frexp(amax / 6.0)
        byte = np.where(mant > 0.5, ex, ex - 1) + 127
    byte = np.clip(np.where(amax > 0, byte, 1), 1, 254)
    scaled = (w * np.exp2(127.0 - byte)[:, None, :]).reshape(k, n).astype(np.float32)
    by_word = np.ascontiguousarray(scaled.reshape(k // 512, 128, 4, n).transpose(0, 1, 3, 2))
    if fmt == "e4m3":
        words = by_word.astype(ml_dtypes.float8_e4m3fn).view(np.uint8)
    else:
        c = by_word.astype(ml_dtypes.float4_e2m1fn).view(np.uint8) & 0xF
        words = (c[..., 0::2] | (c[..., 1::2] << 4)).reshape(k // 512, 128, 2 * n)
    return np.ascontiguousarray(words), np.ascontiguousarray(byte.astype(np.uint8).reshape(k // 512, 16, n))


def unpack_weight(words, scales, fmt):
    g, _, n = scales.shape
    words = np.ascontiguousarray(words).reshape(g, 128, n, -1)
    if fmt == "e4m3":
        vals = words.view(ml_dtypes.float8_e4m3fn).astype(np.float64)
    else:
        nib = np.empty((g, 128, n, 4), np.uint8)
        nib[..., 0::2] = words & 0xF
        nib[..., 1::2] = words >> 4
        vals = E2M1[nib]
    vals = vals * np.repeat(np.exp2(scales.astype(np.float64) - 127.0), 8, axis=1)[..., None]
    return vals.transpose(0, 1, 3, 2).reshape(g * 512, n)


def relu2(v):
    return np.maximum(v, 0.0) ** 2


K, T, E, C, N = 1024, 1280, 16, 128, 128
PAD = 32
K8 = 512


def by_expert(wq, xq):
    return np.concatenate([wq[e].T @ xq[:, e * C:(e + 1) * C] for e in range(E)], axis=1)


def setup_inputs():
    n = np.random.standard_normal
    s = mx_kscale(K)[:, None]
    first = np.random.permutation(np.repeat(np.arange(E), T // E))
    second = (first + 1 + np.random.permutation(np.repeat(np.arange(E - 1), -(-T // (E - 1)))[:T])) % E
    while np.bincount(second, minlength=E).max() != T // E:
        load = np.bincount(second, minlength=E); hi, lo = int(load.argmax()), int(load.argmin())
        t = np.flatnonzero((second == hi) & (first != lo))[0]; second[t] = lo
    slot_token = np.empty(E * C, np.int64); pos = np.empty((2, T), np.int64); fill = np.zeros(E, np.int64)
    place = np.stack([np.random.permutation(C) for _ in range(E)])
    for r, deal in enumerate((first, second)):
        for t in np.random.permutation(T):
            e = deal[t]
            if fill[e] < C: j = e * C + place[e, fill[e]]; fill[e] += 1; slot_token[j] = t; pos[r, t] = j
            else: pos[r, t] = E * C + t % PAD
    g = np.random.uniform(0.2, 0.8, T)
    w = n((E, K, N)) / np.sqrt(K) / s[None]
    w8 = [pack_weight(m[:K8], "e4m3") for m in w]
    w4 = [pack_weight(m[K8:], "e2m1") for m in w]
    return {
        "xT": (n((K, T)) * s).astype(np.float32),
        "w8_words": np.stack([m[0] for m in w8]),
        "w8_scales": np.stack([m[1] for m in w8]),
        "w4_words": np.stack([m[0] for m in w4]),
        "w4_scales": np.stack([m[1] for m in w4]),
        "b": (0.3 * n((N, E))).astype(np.float32),
        "gate": np.stack([np.tile(g, (N, 1)), np.tile(1.0 - g, (N, 1))]).astype(np.float32),
        "offs": striped(slot_token),
        "pos1": striped(pos[0]),
        "pos2": striped(pos[1]),
    }


def reference(xT, w8_words, w8_scales, w4_words, w4_scales, b, gate, offs, pos1, pos2):
    idx = unstriped(offs)
    w = np.stack([np.concatenate([unpack_weight(w8_words[e], w8_scales[e], "e4m3"), unpack_weight(w4_words[e], w4_scales[e], "e2m1")]) for e in range(E)])
    xq = mxq(f64(xT)[:, idx], 0, "e4m3")
    y = by_expert(w, xq)
    y = relu2(y + np.repeat(f64(b), C, axis=1))
    y = np.concatenate([y, np.zeros((N, PAD))], axis=1)
    return f64(gate[0]) * y[:, unstriped(pos1)] + f64(gate[1]) * y[:, unstriped(pos2)]

@@ -1,0 +1,202 @@
+from contextlib import ExitStack
+
+import concourse.mybir as mybir
+
+P = 128
+TOKENS = 1280
+EXPERTS = 16
+CAP = 128
+SLOTS = EXPERTS * CAP
+N = 128
+PAD = 32
+K_PASS = 512
+FLOPS = 2 * SLOTS * 2 * K_PASS * N
+
+F32 = mybir.dt.float32
+BF16 = mybir.dt.bfloat16
+U32 = mybir.dt.uint32
+I32 = mybir.dt.int32
+U16 = mybir.dt.uint16
+U8 = mybir.dt.uint8
+FP8X4 = mybir.dt.float8_e4m3fn_x4
+FP4X4 = mybir.dt.float4_e2m1fn_x4
+MULT = mybir.AluOpType.mult
+ADD = mybir.AluOpType.add
+MAX = mybir.AluOpType.max
+RELU = mybir.ActivationFunctionType.Relu
+SQUARE = mybir.ActivationFunctionType.Square
+
+UNIT = 256
+X_LOADS = ((0, 512), (512, 1024), (1024, 1280)), ((0, 256), (256, 512), (512, 768), (768, 1024), (1024, 1280))
+VECTOR_UNITS = ((1, 3, 4), (3,))
+ROW0 = (4, 0)
+GROUPS = ((0, 2), (2, 6), (6, 10), (10, 14), (14, 15), (15, 16))
+ON_VECTOR = 14
+
+
+def tile_moe_cap2_lin_relu2_kernel(
+    tc, xT, w8_words, w8_scales, w4_words, w4_scales, b, gate, offs, pos1, pos2, out
+):
+    nc = tc.nc
+    with ExitStack() as ctx:
+        keep = ctx.enter_context(tc.tile_pool(name="keep", bufs=1))
+        psum = ctx.enter_context(tc.psum_pool(name="psum", bufs=1))
+
+        offs_t = keep.tile([P, SLOTS // 16], U16, name="offs_t")
+        pos1_t = keep.tile([P, TOKENS // 16], U16, name="pos1_t")
+        pos2_t = keep.tile([P, TOKENS // 16], U16, name="pos2_t")
+        bias_t = keep.tile([P, EXPERTS], F32, name="bias_t")
+        gate_t = [keep.tile([P, TOKENS], F32, name=f"gate{c}") for c in range(2)]
+        w8_t = keep.tile([P, EXPERTS * 4 * N], U8, name="w8_t", align_bytes=64)
+        w4_t = keep.tile([P, EXPERTS * 2 * N], U8, name="w4_t", align_bytes=64)
+        ws_t = keep.tile([P, EXPERTS * N], U8, name="ws_t", align_bytes=64)
+        codes = [keep.tile([P, TOKENS], U32, name=f"codes{a}", align_bytes=64) for a in range(2)]
+        scales = keep.tile([P, TOKENS], U8, name="scales", align_bytes=64)
+        slot_codes = [keep.tile([P, SLOTS], U32, name=f"slot_codes{a}", align_bytes=64) for a in range(2)]
+        slot_scales = keep.tile([P, SLOTS], U8, name="slot_scales", align_bytes=64)
+        y = keep.tile([P, SLOTS + PAD], F32, name="y")
+
+        nc.vector.memset(ws_t[:].bitcast(I32), 0)
+        nc.gpsimd.memset(scales[:], 0)
+        nc.gpsimd.memset(y[:, SLOTS:], 0.0)
+        ws_i32 = ws_t[:].bitcast(I32).rearrange("p (e n) -> p e n", e=EXPERTS)
+        for row0, src in ((ROW0[0], w8_scales), (ROW0[1], w4_scales)):
+            rows = src.rearrange("e a q n -> q (e a) n").bitcast(I32)
+            for quad in range(4):
+                nc.scalar.dma_start(
+                    ws_i32[32 * quad + row0 : 32 * quad + row0 + 4], rows[4 * quad : 4 * quad + 4]
+                )
+
+        x_raw = [[], []]
+
+        def load_x(a):
+            rows = xT[a * K_PASS : (a + 1) * K_PASS, :].rearrange("(p j) t -> p j t", j=4)
+            for lo, hi in X_LOADS[a]:
+                raw = keep.tile([P, 4, hi - lo], F32, name=f"raw{a}_{lo}")
+                nc.sync.dma_start(raw[:], rows[:, :, lo:hi])
+                for u in range(lo, hi, UNIT):
+                    x_raw[a].append(raw[:, :, u - lo : u - lo + UNIT])
+
+        load_x(0)
+        nc.sync.dma_start(offs_t[:], offs)
+        nc.sync.dma_start(bias_t[:], b)
+        load_x(1)
+        w8_dst = w8_t[:].bitcast(I32).rearrange("p (e n) -> p e n", e=EXPERTS)
+        w4_dst = w4_t[:].bitcast(I32).rearrange("p (e n) -> p e n", e=EXPERTS)
+        w8_src = w8_words.rearrange("e a p n r -> p (e a) (n r)").bitcast(I32)
+        w4_src = w4_words.rearrange("e a p n -> p (e a) n").bitcast(I32)
+        for lo in range(0, EXPERTS, 4):
+            nc.sync.dma_start(w8_dst[:, lo : lo + 4], w8_src[:, lo : lo + 4])
+            nc.sync.dma_start(w4_dst[:, lo : lo + 4], w4_src[:, lo : lo + 4])
+        nc.sync.dma_start(pos1_t[:], pos1)
+        nc.sync.dma_start(pos2_t[:], pos2)
+        for c in range(2):
+            nc.sync.dma_start(gate_t[c][:], gate[c])
+
+        def interleave(a, u):
+            grouped = keep.tile([P, UNIT, 4], BF16, name=f"grouped{a}_{u}", align_bytes=64)
+            src = x_raw[a][u].rearrange("p j t -> p t j")
+            if u in VECTOR_UNITS[a]:
+                nc.vector.tensor_copy(grouped[:], src)
+            else:
+                nc.scalar.copy(grouped[:], src)
+            return grouped
+
+        def quantize(a, u, grouped):
+            cols = slice(u * UNIT, (u + 1) * UNIT)
+            nc.vector.quantize_mx(
+                out=codes[a][:, cols].bitcast(FP8X4),
+                scales=scales[ROW0[a] :, cols],
+                in_=grouped[:].rearrange("p t j -> p (t j)"),
+            )
+
+        def gather(dst, window, lo, hi):
+            nc.vector.tensor_copy(dst[:, lo:hi], window[:].indirect(offs_t[:, lo // 16 : hi // 16]))
+
+        units = range(TOKENS // UNIT)
+        g0 = [interleave(0, u) for u in units]
+        for u in units:
+            quantize(0, u, g0[u])
+        g1 = {u: interleave(1, u) for u in units if u not in VECTOR_UNITS[1]}
+        gather(slot_codes[0], codes[0], 0, 768)
+        quantize(1, 0, g1[0])
+        gather(slot_codes[0], codes[0], 768, 1536)
+        quantize(1, 1, g1[1])
+        gather(slot_codes[0], codes[0], 1536, 2048)
+        for u in VECTOR_UNITS[1]:
+            g1[u] = interleave(1, u)
+        for u in (2, 3, 4):
+            quantize(1, u, g1[u])
+
+        banks = {lo: psum.tile([P, (hi - lo) * CAP], F32, name=f"bank{lo}") for lo, hi in GROUPS}
+        where = {e: banks[lo][:, (e - lo) * CAP : (e - lo + 1) * CAP] for lo, hi in GROUPS for e in range(lo, hi)}
+
+        def expert(e):
+            cols = slice(e * CAP, (e + 1) * CAP)
+            acc = where[e]
+            nc.tensor.matmul_mx(
+                out=acc,
+                lhsT=w8_t[:, e * 4 * N : (e + 1) * 4 * N].bitcast(FP8X4),
+                lhsT_scale=ws_t[ROW0[0] :, e * N : (e + 1) * N],
+                rhs=slot_codes[0][:, cols].bitcast(FP8X4),
+                rhs_scale=slot_scales[ROW0[0] :, cols],
+                start=True,
+                stop=False,
+            )
+            nc.tensor.matmul_mx(
+                out=acc,
+                lhsT=w4_t[:, e * 2 * N : (e + 1) * 2 * N].bitcast(FP4X4),
+                lhsT_scale=ws_t[:, e * N : (e + 1) * N],
+                rhs=slot_codes[1][:, cols].bitcast(FP8X4),
+                rhs_scale=slot_scales[:, cols],
+                start=False,
+                stop=True,
+            )
+
+        def activate(lo, hi):
+            r = keep.tile([P, (hi - lo) * CAP], F32, name=f"r{lo}")
+            for e in range(lo, hi):
+                nc.scalar.activation(
+                    r[:, (e - lo) * CAP : (e - lo + 1) * CAP],
+                    where[e],
+                    RELU,
+                    bias=bias_t[:, e : e + 1],
+                )
+            nc.scalar.activation(y[:, lo * CAP : hi * CAP], r[:], SQUARE)
+
+        def activate_vector(lo, hi):
+            r = keep.tile([P, (hi - lo) * CAP], F32, name=f"r{lo}")
+            for e in range(lo, hi):
+                nc.vector.tensor_scalar(
+                    r[:, (e - lo) * CAP : (e - lo + 1) * CAP], where[e], bias_t[:, e : e + 1], 0.0, ADD, MAX
+                )
+            nc.vector.tensor_tensor(y[:, lo * CAP : hi * CAP], r[:], r[:], MULT)
+
+        for lo, hi in ((0, 2), (2, 6), (6, 10), (10, 16)):
+            gather(slot_codes[1], codes[1], lo * CAP, hi * CAP)
+            for a, z in ((lo, hi),) if hi < EXPERTS else ((lo, ON_VECTOR), (ON_VECTOR, hi)):
+                gather(slot_scales, scales, a * CAP, z * CAP)
+                for e in range(a, z):
+                    expert(e)
+                if a < ON_VECTOR:
+                    activate(a, z)
+        activate_vector(ON_VECTOR, EXPERTS)
+
+        def product(c, pos, lo, hi):
+            z = keep.tile([P, hi - lo], F32, name=f"z{c}_{lo}")
+            nc.vector.tensor_tensor(z[:], y[:].indirect(pos[:, lo // 16 : hi // 16]), gate_t[c][:, lo:hi], MULT)
+            return z
+
+        def finish(lo, hi, z1, z2):
+            o = keep.tile([P, hi - lo], F32, name=f"o{lo}")
+            nc.vector.tensor_tensor(o[:], z1[:], z2[:], ADD)
+            nc.sync.dma_start(out[:, lo:hi], o[:])
+
+        pending = None
+        for lo, hi in ((0, 640), (640, 1024), (1024, 1280)):
+            z1 = product(0, pos1_t, lo, hi)
+            if pending is not None:
+                finish(*pending)
+            z2 = product(1, pos2_t, lo, hi)
+            pending = (lo, hi, z1, z2)
+        finish(*pending)

@@ -27,10 +27,10 @@ RELU = mybir.ActivationFunctionType.Relu
 SQUARE = mybir.ActivationFunctionType.Square
 
 UNIT = 256
-X_LOADS = ((0, 512), (512, 1024), (1024, 1280)), ((0, 256), (256, 512), (512, 768), (768, 1024), (1024, 1280))
-VECTOR_UNITS = ((1, 3, 4), (3,))
+X_LOADS = ((0, 512), (512, 1024), (1024, 1280))
+VECTOR_UNITS = ((1, 3, 4), (3, 4))
 ROW0 = (4, 0)
-GROUPS = ((0, 2), (2, 6), (6, 10), (10, 14), (14, 15), (15, 16))
+GROUPS = ((0, 2), (2, 6), (6, 10), (10, 12), (12, 14), (14, 15), (15, 16))
 ON_VECTOR = 14
 
 
@@ -58,20 +58,21 @@ def tile_moe_cap2_lin_relu2_kernel(
 
         nc.vector.memset(ws_t[:].bitcast(I32), 0)
         nc.gpsimd.memset(scales[:], 0)
-        nc.gpsimd.memset(y[:, SLOTS:], 0.0)
         ws_i32 = ws_t[:].bitcast(I32).rearrange("p (e n) -> p e n", e=EXPERTS)
-        for row0, src in ((ROW0[0], w8_scales), (ROW0[1], w4_scales)):
+
+        def load_scale_rows(queue, row0, src):
             rows = src.rearrange("e a q n -> q (e a) n").bitcast(I32)
             for quad in range(4):
-                nc.scalar.dma_start(
-                    ws_i32[32 * quad + row0 : 32 * quad + row0 + 4], rows[4 * quad : 4 * quad + 4]
-                )
+                queue.dma_start(ws_i32[32 * quad + row0 : 32 * quad + row0 + 4], rows[4 * quad : 4 * quad + 4])
+
+        load_scale_rows(nc.gpsimd, ROW0[0], w8_scales)
+        nc.gpsimd.memset(y[:, SLOTS:], 0.0)
 
         x_raw = [[], []]
 
         def load_x(a):
             rows = xT[a * K_PASS : (a + 1) * K_PASS, :].rearrange("(p j) t -> p j t", j=4)
-            for lo, hi in X_LOADS[a]:
+            for lo, hi in X_LOADS:
                 raw = keep.tile([P, 4, hi - lo], F32, name=f"raw{a}_{lo}")
                 nc.sync.dma_start(raw[:], rows[:, :, lo:hi])
                 for u in range(lo, hi, UNIT):
@@ -79,8 +80,8 @@ def tile_moe_cap2_lin_relu2_kernel(
 
         load_x(0)
         nc.sync.dma_start(offs_t[:], offs)
-        nc.sync.dma_start(bias_t[:], b)
         load_x(1)
+        load_scale_rows(nc.sync, ROW0[1], w4_scales)
         w8_dst = w8_t[:].bitcast(I32).rearrange("p (e n) -> p e n", e=EXPERTS)
         w4_dst = w4_t[:].bitcast(I32).rearrange("p (e n) -> p e n", e=EXPERTS)
         w8_src = w8_words.rearrange("e a p n r -> p (e a) (n r)").bitcast(I32)
@@ -88,6 +89,8 @@ def tile_moe_cap2_lin_relu2_kernel(
         for lo in range(0, EXPERTS, 4):
             nc.sync.dma_start(w8_dst[:, lo : lo + 4], w8_src[:, lo : lo + 4])
             nc.sync.dma_start(w4_dst[:, lo : lo + 4], w4_src[:, lo : lo + 4])
+            if lo == 0:
+                nc.sync.dma_start(bias_t[:], b)
         nc.sync.dma_start(pos1_t[:], pos1)
         nc.sync.dma_start(pos2_t[:], pos2)
         for c in range(2):
@@ -172,14 +175,13 @@ def tile_moe_cap2_lin_relu2_kernel(
                 )
             nc.vector.tensor_tensor(y[:, lo * CAP : hi * CAP], r[:], r[:], MULT)
 
-        for lo, hi in ((0, 2), (2, 6), (6, 10), (10, 16)):
+        for lo, hi in ((0, 2), (2, 6), (6, 10), (10, 12), (12, 14), (14, 16)):
             gather(slot_codes[1], codes[1], lo * CAP, hi * CAP)
-            for a, z in ((lo, hi),) if hi < EXPERTS else ((lo, ON_VECTOR), (ON_VECTOR, hi)):
-                gather(slot_scales, scales, a * CAP, z * CAP)
-                for e in range(a, z):
-                    expert(e)
-                if a < ON_VECTOR:
-                    activate(a, z)
+            gather(slot_scales, scales, lo * CAP, hi * CAP)
+            for e in range(lo, hi):
+                expert(e)
+            if lo < ON_VECTOR:
+                activate(lo, hi)
         activate_vector(ON_VECTOR, EXPERTS)
 
         def product(c, pos, lo, hi):

@@ -28,10 +28,17 @@ SQUARE = mybir.ActivationFunctionType.Square
 
 UNIT = 256
 X_LOADS = ((0, 512), (512, 1024), (1024, 1280))
-VECTOR_UNITS = ((1, 3, 4), (3, 4))
+VECTOR_COLS = (
+    ((256, 512), (768, 1024), (1024, 1184)),
+    ((768, 1024), (1024, 1184)),
+)
+SCALAR_COLS = (
+    ((0, 256), (512, 768), (1184, 1280)),
+    ((0, 256), (256, 512), (512, 768), (1184, 1280)),
+)
 ROW0 = (4, 0)
-GROUPS = ((0, 2), (2, 6), (6, 10), (10, 12), (12, 14), (14, 15), (15, 16))
-ON_VECTOR = 14
+GROUPS = ((0, 2), (2, 6), (6, 10), (10, 12), (12, 13), (13, 14), (14, 15), (15, 16))
+ON_VECTOR = 13
 
 
 def tile_moe_cap2_lin_relu2_kernel(
@@ -68,15 +75,15 @@ def tile_moe_cap2_lin_relu2_kernel(
         load_scale_rows(nc.gpsimd, ROW0[0], w8_scales)
         nc.gpsimd.memset(y[:, SLOTS:], 0.0)
 
-        x_raw = [[], []]
+        x_raw = [
+            {lo: keep.tile([P, 4, hi - lo], F32, name=f"raw{a}_{lo}") for lo, hi in X_LOADS} for a in range(2)
+        ]
+        grouped = [keep.tile([P, TOKENS, 4], BF16, name=f"grouped{a}", align_bytes=64) for a in range(2)]
 
         def load_x(a):
             rows = xT[a * K_PASS : (a + 1) * K_PASS, :].rearrange("(p j) t -> p j t", j=4)
             for lo, hi in X_LOADS:
-                raw = keep.tile([P, 4, hi - lo], F32, name=f"raw{a}_{lo}")
-                nc.sync.dma_start(raw[:], rows[:, :, lo:hi])
-                for u in range(lo, hi, UNIT):
-                    x_raw[a].append(raw[:, :, u - lo : u - lo + UNIT])
+                nc.sync.dma_start(x_raw[a][lo][:], rows[:, :, lo:hi])
 
         load_x(0)
         nc.sync.dma_start(offs_t[:], offs)
@@ -96,40 +103,38 @@ def tile_moe_cap2_lin_relu2_kernel(
         for c in range(2):
             nc.sync.dma_start(gate_t[c][:], gate[c])
 
-        def interleave(a, u):
-            grouped = keep.tile([P, UNIT, 4], BF16, name=f"grouped{a}_{u}", align_bytes=64)
-            src = x_raw[a][u].rearrange("p j t -> p t j")
-            if u in VECTOR_UNITS[a]:
-                nc.vector.tensor_copy(grouped[:], src)
-            else:
-                nc.scalar.copy(grouped[:], src)
-            return grouped
+        def interleave(a, copy, cols):
+            for lo, hi in cols:
+                start = max(first for first, last in X_LOADS if first <= lo)
+                copy(
+                    grouped[a][:, lo:hi, :].rearrange("p (c i) j -> p c j i", i=4),
+                    x_raw[a][start][:, :, lo - start : hi - start].rearrange("p j (c i) -> p c j i", i=4),
+                )
 
-        def quantize(a, u, grouped):
+        def quantize(a, u):
             cols = slice(u * UNIT, (u + 1) * UNIT)
             nc.vector.quantize_mx(
                 out=codes[a][:, cols].bitcast(FP8X4),
                 scales=scales[ROW0[a] :, cols],
-                in_=grouped[:].rearrange("p t j -> p (t j)"),
+                in_=grouped[a][:, cols, :].rearrange("p t j -> p (t j)"),
             )
 
         def gather(dst, window, lo, hi):
             nc.vector.tensor_copy(dst[:, lo:hi], window[:].indirect(offs_t[:, lo // 16 : hi // 16]))
 
-        units = range(TOKENS // UNIT)
-        g0 = [interleave(0, u) for u in units]
-        for u in units:
-            quantize(0, u, g0[u])
-        g1 = {u: interleave(1, u) for u in units if u not in VECTOR_UNITS[1]}
+        interleave(0, nc.scalar.copy, SCALAR_COLS[0])
+        interleave(0, nc.vector.tensor_copy, VECTOR_COLS[0])
+        for u in range(TOKENS // UNIT):
+            quantize(0, u)
+        interleave(1, nc.scalar.copy, SCALAR_COLS[1])
         gather(slot_codes[0], codes[0], 0, 768)
-        quantize(1, 0, g1[0])
+        quantize(1, 0)
         gather(slot_codes[0], codes[0], 768, 1536)
-        quantize(1, 1, g1[1])
+        quantize(1, 1)
         gather(slot_codes[0], codes[0], 1536, 2048)
-        for u in VECTOR_UNITS[1]:
-            g1[u] = interleave(1, u)
+        interleave(1, nc.vector.tensor_copy, VECTOR_COLS[1])
         for u in (2, 3, 4):
-            quantize(1, u, g1[u])
+            quantize(1, u)
 
         banks = {lo: psum.tile([P, (hi - lo) * CAP], F32, name=f"bank{lo}") for lo, hi in GROUPS}
         where = {e: banks[lo][:, (e - lo) * CAP : (e - lo + 1) * CAP] for lo, hi in GROUPS for e in range(lo, hi)}
@@ -181,8 +186,9 @@ def tile_moe_cap2_lin_relu2_kernel(
             for e in range(lo, hi):
                 expert(e)
             if lo < ON_VECTOR:
-                activate(lo, hi)
-        activate_vector(ON_VECTOR, EXPERTS)
+                activate(lo, min(hi, ON_VECTOR))
+        activate_vector(ON_VECTOR, EXPERTS - 1)
+        activate_vector(EXPERTS - 1, EXPERTS)
 
         def product(c, pos, lo, hi):
             z = keep.tile([P, hi - lo], F32, name=f"z{c}_{lo}")

@@ -98,10 +98,12 @@ def tile_moe_cap2_lin_relu2_kernel(
             nc.sync.dma_start(w4_dst[:, lo : lo + 4], w4_src[:, lo : lo + 4])
             if lo == 0:
                 nc.sync.dma_start(bias_t[:], b)
-        nc.sync.dma_start(pos1_t[:], pos1)
+            if lo == 4:
+                nc.sync.dma_start(pos1_t[:], pos1)
+            if lo == 8:
+                nc.sync.dma_start(gate_t[0][:], gate[0])
         nc.sync.dma_start(pos2_t[:], pos2)
-        for c in range(2):
-            nc.sync.dma_start(gate_t[c][:], gate[c])
+        nc.sync.dma_start(gate_t[1][:], gate[1])
 
         def interleave(a, copy, cols):
             for lo, hi in cols:
@@ -139,26 +141,20 @@ def tile_moe_cap2_lin_relu2_kernel(
         banks = {lo: psum.tile([P, (hi - lo) * CAP], F32, name=f"bank{lo}") for lo, hi in GROUPS}
         where = {e: banks[lo][:, (e - lo) * CAP : (e - lo + 1) * CAP] for lo, hi in GROUPS for e in range(lo, hi)}
 
-        def expert(e):
+        def multiply(e, a):
             cols = slice(e * CAP, (e + 1) * CAP)
-            acc = where[e]
+            if a == 0:
+                weights = w8_t[:, e * 4 * N : (e + 1) * 4 * N].bitcast(FP8X4)
+            else:
+                weights = w4_t[:, e * 2 * N : (e + 1) * 2 * N].bitcast(FP4X4)
             nc.tensor.matmul_mx(
-                out=acc,
-                lhsT=w8_t[:, e * 4 * N : (e + 1) * 4 * N].bitcast(FP8X4),
-                lhsT_scale=ws_t[ROW0[0] :, e * N : (e + 1) * N],
-                rhs=slot_codes[0][:, cols].bitcast(FP8X4),
-                rhs_scale=slot_scales[ROW0[0] :, cols],
-                start=True,
-                stop=False,
-            )
-            nc.tensor.matmul_mx(
-                out=acc,
-                lhsT=w4_t[:, e * 2 * N : (e + 1) * 2 * N].bitcast(FP4X4),
-                lhsT_scale=ws_t[:, e * N : (e + 1) * N],
-                rhs=slot_codes[1][:, cols].bitcast(FP8X4),
-                rhs_scale=slot_scales[:, cols],
-                start=False,
-                stop=True,
+                out=where[e],
+                lhsT=weights,
+                lhsT_scale=ws_t[ROW0[a] :, e * N : (e + 1) * N],
+                rhs=slot_codes[a][:, cols].bitcast(FP8X4),
+                rhs_scale=slot_scales[ROW0[a] :, cols],
+                start=(a == 0),
+                stop=(a == 1),
             )
 
         def activate(lo, hi):
@@ -181,30 +177,35 @@ def tile_moe_cap2_lin_relu2_kernel(
             nc.vector.tensor_tensor(y[:, lo * CAP : hi * CAP], r[:], r[:], MULT)
 
         for lo, hi in ((0, 2), (2, 6), (6, 10), (10, 12), (12, 14), (14, 16)):
-            gather(slot_codes[1], codes[1], lo * CAP, hi * CAP)
             gather(slot_scales, scales, lo * CAP, hi * CAP)
-            for e in range(lo, hi):
-                expert(e)
+            gather(slot_codes[1], codes[1], lo * CAP, hi * CAP)
+            order = [(e, a) for e in range(lo, hi) for a in range(2)]
+            if lo >= 12:
+                order = [(e, a) for a in range(2) for e in range(lo, hi)]
+            for e, a in order:
+                multiply(e, a)
             if lo < ON_VECTOR:
                 activate(lo, min(hi, ON_VECTOR))
         activate_vector(ON_VECTOR, EXPERTS - 1)
         activate_vector(EXPERTS - 1, EXPERTS)
 
-        def product(c, pos, lo, hi):
-            z = keep.tile([P, hi - lo], F32, name=f"z{c}_{lo}")
-            nc.vector.tensor_tensor(z[:], y[:].indirect(pos[:, lo // 16 : hi // 16]), gate_t[c][:, lo:hi], MULT)
-            return z
+        z1 = keep.tile([P, TOKENS], F32, name="z1")
+        nc.vector.tensor_tensor(z1[:], y[:].indirect(pos1_t[:]), gate_t[0][:], MULT)
+        z2 = keep.tile([P, TOKENS], F32, name="z2")
+        o = keep.tile([P, TOKENS], F32, name="o")
 
-        def finish(lo, hi, z1, z2):
-            o = keep.tile([P, hi - lo], F32, name=f"o{lo}")
-            nc.vector.tensor_tensor(o[:], z1[:], z2[:], ADD)
-            nc.sync.dma_start(out[:, lo:hi], o[:])
+        def product(lo, hi):
+            nc.vector.tensor_tensor(
+                z2[:, lo:hi], y[:].indirect(pos2_t[:, lo // 16 : hi // 16]), gate_t[1][:, lo:hi], MULT
+            )
 
-        pending = None
-        for lo, hi in ((0, 640), (640, 1024), (1024, 1280)):
-            z1 = product(0, pos1_t, lo, hi)
-            if pending is not None:
-                finish(*pending)
-            z2 = product(1, pos2_t, lo, hi)
-            pending = (lo, hi, z1, z2)
-        finish(*pending)
+        def finish(lo, hi):
+            nc.vector.tensor_tensor(o[:, lo:hi], z1[:, lo:hi], z2[:, lo:hi], ADD)
+            nc.sync.dma_start(out[:, lo:hi], o[:, lo:hi])
+
+        product(0, 704)
+        product(704, 1088)
+        finish(0, 704)
+        product(1088, 1280)
+        finish(704, 1088)
+        finish(1088, 1280)

from contextlib import ExitStack

import concourse.mybir as mybir

P = 128
TOKENS = 1280
EXPERTS = 16
CAP = 128
SLOTS = EXPERTS * CAP
N = 128
PAD = 32
K_PASS = 512
FLOPS = 2 * SLOTS * 2 * K_PASS * N

F32 = mybir.dt.float32
BF16 = mybir.dt.bfloat16
U32 = mybir.dt.uint32
I32 = mybir.dt.int32
U16 = mybir.dt.uint16
U8 = mybir.dt.uint8
FP8X4 = mybir.dt.float8_e4m3fn_x4
FP4X4 = mybir.dt.float4_e2m1fn_x4
MULT = mybir.AluOpType.mult
ADD = mybir.AluOpType.add
MAX = mybir.AluOpType.max
RELU = mybir.ActivationFunctionType.Relu
SQUARE = mybir.ActivationFunctionType.Square

UNIT = 256
X_LOADS = ((0, 512), (512, 1024), (1024, 1280))
VECTOR_COLS = (
    ((256, 512), (768, 1024), (1024, 1184)),
    ((768, 1024), (1024, 1184)),
)
SCALAR_COLS = (
    ((0, 256), (512, 768), (1184, 1280)),
    ((0, 256), (256, 512), (512, 768), (1184, 1280)),
)
ROW0 = (4, 0)
GROUPS = ((0, 2), (2, 6), (6, 10), (10, 12), (12, 13), (13, 14), (14, 15), (15, 16))
ON_VECTOR = 13


def tile_moe_cap2_lin_relu2_kernel(
    tc, xT, w8_words, w8_scales, w4_words, w4_scales, b, gate, offs, pos1, pos2, out
):
    nc = tc.nc
    with ExitStack() as ctx:
        keep = ctx.enter_context(tc.tile_pool(name="keep", bufs=1))
        psum = ctx.enter_context(tc.psum_pool(name="psum", bufs=1))

        offs_t = keep.tile([P, SLOTS // 16], U16, name="offs_t")
        pos1_t = keep.tile([P, TOKENS // 16], U16, name="pos1_t")
        pos2_t = keep.tile([P, TOKENS // 16], U16, name="pos2_t")
        bias_t = keep.tile([P, EXPERTS], F32, name="bias_t")
        gate_t = [keep.tile([P, TOKENS], F32, name=f"gate{c}") for c in range(2)]
        w8_t = keep.tile([P, EXPERTS * 4 * N], U8, name="w8_t", align_bytes=64)
        w4_t = keep.tile([P, EXPERTS * 2 * N], U8, name="w4_t", align_bytes=64)
        ws_t = keep.tile([P, EXPERTS * N], U8, name="ws_t", align_bytes=64)
        codes = [keep.tile([P, TOKENS], U32, name=f"codes{a}", align_bytes=64) for a in range(2)]
        scales = keep.tile([P, TOKENS], U8, name="scales", align_bytes=64)
        slot_codes = [keep.tile([P, SLOTS], U32, name=f"slot_codes{a}", align_bytes=64) for a in range(2)]
        slot_scales = keep.tile([P, SLOTS], U8, name="slot_scales", align_bytes=64)
        y = keep.tile([P, SLOTS + PAD], F32, name="y")

        nc.vector.memset(ws_t[:].bitcast(I32), 0)
        nc.gpsimd.memset(scales[:], 0)
        ws_i32 = ws_t[:].bitcast(I32).rearrange("p (e n) -> p e n", e=EXPERTS)

        def load_scale_rows(queue, row0, src):
            rows = src.rearrange("e a q n -> q (e a) n").bitcast(I32)
            for quad in range(4):
                queue.dma_start(ws_i32[32 * quad + row0 : 32 * quad + row0 + 4], rows[4 * quad : 4 * quad + 4])

        load_scale_rows(nc.gpsimd, ROW0[0], w8_scales)
        nc.gpsimd.memset(y[:, SLOTS:], 0.0)

        x_raw = [
            {lo: keep.tile([P, 4, hi - lo], F32, name=f"raw{a}_{lo}") for lo, hi in X_LOADS} for a in range(2)
        ]
        grouped = [keep.tile([P, TOKENS, 4], BF16, name=f"grouped{a}", align_bytes=64) for a in range(2)]

        def load_x(a):
            rows = xT[a * K_PASS : (a + 1) * K_PASS, :].rearrange("(p j) t -> p j t", j=4)
            for lo, hi in X_LOADS:
                nc.sync.dma_start(x_raw[a][lo][:], rows[:, :, lo:hi])

        load_x(0)
        nc.sync.dma_start(offs_t[:], offs)
        load_x(1)
        load_scale_rows(nc.sync, ROW0[1], w4_scales)
        w8_dst = w8_t[:].bitcast(I32).rearrange("p (e n) -> p e n", e=EXPERTS)
        w4_dst = w4_t[:].bitcast(I32).rearrange("p (e n) -> p e n", e=EXPERTS)
        w8_src = w8_words.rearrange("e a p n r -> p (e a) (n r)").bitcast(I32)
        w4_src = w4_words.rearrange("e a p n -> p (e a) n").bitcast(I32)
        for lo in range(0, EXPERTS, 4):
            nc.sync.dma_start(w8_dst[:, lo : lo + 4], w8_src[:, lo : lo + 4])
            nc.sync.dma_start(w4_dst[:, lo : lo + 4], w4_src[:, lo : lo + 4])
            if lo == 0:
                nc.sync.dma_start(bias_t[:], b)
            if lo == 4:
                nc.sync.dma_start(pos1_t[:], pos1)
            if lo == 8:
                nc.sync.dma_start(gate_t[0][:], gate[0])
        nc.sync.dma_start(pos2_t[:], pos2)
        nc.sync.dma_start(gate_t[1][:], gate[1])

        def interleave(a, copy, cols):
            for lo, hi in cols:
                start = max(first for first, last in X_LOADS if first <= lo)
                copy(
                    grouped[a][:, lo:hi, :].rearrange("p (c i) j -> p c j i", i=4),
                    x_raw[a][start][:, :, lo - start : hi - start].rearrange("p j (c i) -> p c j i", i=4),
                )

        def quantize(a, u):
            cols = slice(u * UNIT, (u + 1) * UNIT)
            nc.vector.quantize_mx(
                out=codes[a][:, cols].bitcast(FP8X4),
                scales=scales[ROW0[a] :, cols],
                in_=grouped[a][:, cols, :].rearrange("p t j -> p (t j)"),
            )

        def gather(dst, window, lo, hi):
            nc.vector.tensor_copy(dst[:, lo:hi], window[:].indirect(offs_t[:, lo // 16 : hi // 16]))

        interleave(0, nc.scalar.copy, SCALAR_COLS[0])
        interleave(0, nc.vector.tensor_copy, VECTOR_COLS[0])
        for u in range(TOKENS // UNIT):
            quantize(0, u)
        interleave(1, nc.scalar.copy, SCALAR_COLS[1])
        gather(slot_codes[0], codes[0], 0, 768)
        quantize(1, 0)
        gather(slot_codes[0], codes[0], 768, 1536)
        quantize(1, 1)
        gather(slot_codes[0], codes[0], 1536, 2048)
        interleave(1, nc.vector.tensor_copy, VECTOR_COLS[1])
        for u in (2, 3, 4):
            quantize(1, u)

        banks = {lo: psum.tile([P, (hi - lo) * CAP], F32, name=f"bank{lo}") for lo, hi in GROUPS}
        where = {e: banks[lo][:, (e - lo) * CAP : (e - lo + 1) * CAP] for lo, hi in GROUPS for e in range(lo, hi)}

        def multiply(e, a):
            cols = slice(e * CAP, (e + 1) * CAP)
            if a == 0:
                weights = w8_t[:, e * 4 * N : (e + 1) * 4 * N].bitcast(FP8X4)
            else:
                weights = w4_t[:, e * 2 * N : (e + 1) * 2 * N].bitcast(FP4X4)
            nc.tensor.matmul_mx(
                out=where[e],
                lhsT=weights,
                lhsT_scale=ws_t[ROW0[a] :, e * N : (e + 1) * N],
                rhs=slot_codes[a][:, cols].bitcast(FP8X4),
                rhs_scale=slot_scales[ROW0[a] :, cols],
                start=(a == 0),
                stop=(a == 1),
            )

        def activate(lo, hi):
            r = keep.tile([P, (hi - lo) * CAP], F32, name=f"r{lo}")
            for e in range(lo, hi):
                nc.scalar.activation(
                    r[:, (e - lo) * CAP : (e - lo + 1) * CAP],
                    where[e],
                    RELU,
                    bias=bias_t[:, e : e + 1],
                )
            nc.scalar.activation(y[:, lo * CAP : hi * CAP], r[:], SQUARE)

        def activate_vector(lo, hi):
            r = keep.tile([P, (hi - lo) * CAP], F32, name=f"r{lo}")
            for e in range(lo, hi):
                nc.vector.tensor_scalar(
                    r[:, (e - lo) * CAP : (e - lo + 1) * CAP], where[e], bias_t[:, e : e + 1], 0.0, ADD, MAX
                )
            nc.vector.tensor_tensor(y[:, lo * CAP : hi * CAP], r[:], r[:], MULT)

        for lo, hi in ((0, 2), (2, 6), (6, 10), (10, 12), (12, 14), (14, 16)):
            gather(slot_scales, scales, lo * CAP, hi * CAP)
            gather(slot_codes[1], codes[1], lo * CAP, hi * CAP)
            order = [(e, a) for e in range(lo, hi) for a in range(2)]
            if lo >= 12:
                order = [(e, a) for a in range(2) for e in range(lo, hi)]
            for e, a in order:
                multiply(e, a)
            if lo < ON_VECTOR:
                activate(lo, min(hi, ON_VECTOR))
        activate_vector(ON_VECTOR, EXPERTS - 1)
        activate_vector(EXPERTS - 1, EXPERTS)

        z1 = keep.tile([P, TOKENS], F32, name="z1")
        nc.vector.tensor_tensor(z1[:], y[:].indirect(pos1_t[:]), gate_t[0][:], MULT)
        z2 = keep.tile([P, TOKENS], F32, name="z2")
        o = keep.tile([P, TOKENS], F32, name="o")

        def product(lo, hi):
            nc.vector.tensor_tensor(
                z2[:, lo:hi], y[:].indirect(pos2_t[:, lo // 16 : hi // 16]), gate_t[1][:, lo:hi], MULT
            )

        def finish(lo, hi):
            nc.vector.tensor_tensor(o[:, lo:hi], z1[:, lo:hi], z2[:, lo:hi], ADD)
            nc.sync.dma_start(out[:, lo:hi], o[:, lo:hi])

        product(0, 704)
        product(704, 1088)
        finish(0, 704)
        product(1088, 1280)
        finish(704, 1088)
        finish(1088, 1280)
